import numpy as np, ml_dtypes
CORES = [21,109,149,237,277,365,405,493,150,406]
N = 10
import mx_ref
NC, G = 128, 4
C = np.float32(0.037)
BF = ml_dtypes.bfloat16
def tile(rs):
    return np.stack(rs, axis=2).reshape(128, -1).astype(BF)
def act(Z):
    return [np.maximum(z, 0) * C for z in Z]
def pk(c, s, i=0):
    return (np.ascontiguousarray(c[:, 512 * i:512 * i + 512]), mx_ref.live(s[:, 128 * i:128 * i + 128]))
def inputs(rng, e, E):
    def f(*shape):
        v = (rng.standard_normal(shape, dtype=np.float32) * np.exp2(rng.integers(-2, 3, shape[:-1] + (1,)))).astype(BF)
        return mx_ref.spread((v.astype(np.float32) * np.exp2(rng.integers(-E, E + 1, shape[:-2] + (1, 1))).astype(np.float32)).astype(BF), rng, e)
    def packed(k):
        c = np.zeros((N, 128, k * 512), np.uint8); s = np.zeros((N, 128, k * 128), np.uint8)
        for r in range(N):
            for i in range(k):
                a, b = mx_ref.quantize(f(128, 512)); c[r][:, 512 * i:512 * i + 512] = a; s[r][:, 128 * i:128 * i + 128] = mx_ref.plane(b, rng)
        return c, s
    d = {}
    d["ac"], d["az"] = packed(1)
    d["bc"], d["bs"] = packed(1)
    d["cc"], d["cs"] = packed(1)
    d["x"] = f(N, 128, 4 * NC)
    return d
def setup_inputs(rng):
    return inputs(rng, 0, 0)
def setup_inputs_blocks(rng):
    return inputs(rng, 2, 0)
def setup_inputs_wide(rng):
    return inputs(rng, 0, 4)
def reference(ac, az, bc, bs, cc, cs, x):
    y = np.zeros((N, 128, N * NC), np.float32)
    for r in range(N):
        h = mx_ref.quantize(tile(act([mx_ref.matmul(pk(ac[i], az[i]), mx_ref.quantize(x[r])) for i in range(G)])))
        h = mx_ref.quantize(tile(act([mx_ref.matmul(pk(bc[i], bs[i]), h) for i in range(G)])))
        for j in range(N):
            y[r][:, NC * j:NC * j + NC] = mx_ref.matmul(pk(cc[j], cs[j]), h)
    return {"y": y}

@@ -1,0 +1,355 @@
+from concourse.bass import DstId, RemoteDMATransfer
+from concourse.mybir import dt, AluOpType, ActivationFunctionType
+
+N = 10
+G = 4
+SCALE = 0.037
+SIM_CORES = 512
+
+SCRATCH = {
+    "xt": ("sbuf", [128, 512], "bfloat16"),
+    "gt": ("sbuf", [128, 512], "bfloat16"),
+    "ht": ("sbuf", [128, 512], "bfloat16"),
+    "wA": ("sbuf", [128, 128], "float8_e4m3fn_x4"),
+    "vA": ("sbuf", [128, 256], "uint8"),
+    "wB": ("sbuf", [128, 128], "float8_e4m3fn_x4"),
+    "vB": ("sbuf", [128, 256], "uint8"),
+    "wC": ("sbuf", [128, 256], "float8_e4m3fn_x4"),
+    "vC": ("sbuf", [128, 256], "uint8"),
+    "yb": ("sbuf", [128, 256], "float32"),
+    "qc": ("sbuf", [128, 384], "float8_e4m3fn_x4"),
+    "qs": ("sbuf", [128, 384], "uint8"),
+    "psA": ("psum", [128, 1024], "float32"),
+    "psB": ("psum", [128, 1024], "float32"),
+    "psC": ("psum", [128, 2048], "float32"),
+}
+SEMAPHORES = ["sent", "gA", "gB", "gC", "gpA", "gpC", "lx", "xq", "gq", "hq"]
+for _l, _n in (("A", G), ("B", G), ("C", N)):
+    for _i in range(_n):
+        SCRATCH["d%s%d" % (_l, _i)] = ("dram", [128, 128], "float8_e4m3fn_x4")
+        SCRATCH["e%s%d" % (_l, _i)] = ("dram", [128, 128], "uint8")
+        SEMAPHORES += ["k%s%d" % (_l, _i), "p%s%d" % (_l, _i)]
+for _i in range(G):
+    SEMAPHORES += [_s + str(_i) for _s in ("z", "ga", "yy", "ha", "fA", "vfA", "fB", "vfB")]
+for _i in range(N // 2):
+    SCRATCH["dp%d" % _i] = ("dram", [128, 256], "float8_e4m3fn_x4")
+    SCRATCH["ep%d" % _i] = ("dram", [128, 256], "uint8")
+    SEMAPHORES += [_s + str(_i) for _s in ("cb", "kp", "pp", "fC", "st")]
+for _i in range(N):
+    SEMAPHORES += ["mm%d" % _i, "cp%d" % _i]
+
+ROUTES = [
+    (0, ("at", 2), [2, 8, 1, 3], {0: "AC", 1: "PB"}),
+    (0, ("at", 6), [6, 9, 4, 5, 7], {0: "AC", 1: "PB"}),
+    (2, ("at", 0), [0, 1, 3, 8, 6, 9], {0: "AC", 1: "PB"}),
+    (2, ("at", 4), [4, 5, 7], {0: "AC", 1: "PB"}),
+    (1, ("mate", 2), [2, 8, 3, 0], {0: "AC", 1: "PB"}),
+    (3, ("mate", 2), [2, 8, 1, 0], {3: "AC", 2: "PB"}),
+    (1, ("mate", 6), [6, 9, 7, 5, 4], {0: "A", 1: "P", 2: "C", 3: "B"}),
+    (3, ("at", 5), [5, 7, 4, 6, 9], {0: "A", 1: "P", 3: "BC"}),
+    (4, ("at", 6), [6, 5, 7], {2: "T"}),
+    (4, ("at", 2), [2, 0, 1, 3], {2: "T"}),
+    (6, ("at", 4), [4, 5, 7], {2: "T"}),
+    (6, ("at", 0), [0, 2, 1, 3], {2: "T"}),
+    (5, ("at", 7), [7, 4, 6], {0: "T"}),
+    (5, ("at", 3), [3, 1, 0, 2], {0: "T"}),
+    (7, ("at", 5), [5, 4, 6], {2: "T"}),
+    (7, ("at", 1), [1, 3, 0, 2], {0: "T"}),
+    (8, ("at", 0), [0, 1, 3, 6], {3: "T"}),
+    (8, ("at", 4), [4, 5, 7], {3: "T"}),
+    (9, ("at", 4), [4, 5, 7], {3: "T"}),
+    (9, ("at", 0), [0, 1, 3, 2], {3: "T"}),
+]
+EARLY = {0: [6, 9], 1: [7], 2: [4, 8], 3: [5]}
+ORDER = {0: [0, 2, 1, 3], 1: [1, 3, 0, 2], 2: [2, 0, 1, 3], 3: [3, 1, 0, 2], 8: [2, 0, 1, 3],
+         4: [2, 0, 1, 3], 5: [3, 2, 0, 1], 6: [0, 1, 2, 3], 9: [0, 1, 2, 3], 7: [1, 3, 0, 2]}
+PAIRS = [2, 3, 4, 0, 1]
+ENGINES = 8
+_PLAN = {}
+
+
+def same_chip(topo, a, b):
+    return topo.host(a) == topo.host(b) and topo.chip(a) == topo.chip(b)
+
+
+def site_cores(T, topo, site, served):
+    kind, r = site
+    ref = T.cores[r]
+    cs = [c for c in range(SIM_CORES) if (same_chip(topo, c, ref) if kind == "at" else topo.mates(c, ref))]
+    cs = [c for c in cs if T.rank_of(c) is None and all(topo.may_write(c, T.cores[d]) for d in served)]
+    near = [c for c in cs if topo.die(c) == topo.die(ref)]
+    far = [c for c in cs if topo.die(c) != topo.die(ref)]
+    out = []
+    for i in range(max(len(near), len(far))):
+        out += near[i:i + 1] + far[i:i + 1]
+    return out
+
+
+def plan(T, topo):
+    if _PLAN:
+        return _PLAN
+    hop1, jobs, coll, serves = {}, {}, {}, {}
+    for s, site, dests, lanes in ROUTES:
+        served = set()
+        for r in ROUTES:
+            if r[1] == site:
+                served.update(r[2])
+        cs = site_cores(T, topo, site, served)
+        for n, items in lanes.items():
+            for it in items:
+                hop1.setdefault((s, it), []).append(cs[n])
+                jobs.setdefault(cs[n], []).append((s, it, dests))
+    for r in range(N):
+        here = [q for q in range(N) if same_chip(topo, T.cores[q], T.cores[r])]
+        free = [c for c in site_cores(T, topo, ("at", r), here) if c not in jobs]
+        coll[r] = (free[0], free[1])
+        serves[free[0]] = ("k", here)
+        serves[free[1]] = ("p", here)
+    _PLAN["hop1"] = hop1
+    _PLAN["jobs"] = jobs
+    _PLAN["coll"] = coll
+    _PLAN["serves"] = serves
+    return _PLAN
+
+
+def collectors(T, topo, source, ranks, which):
+    coll, out = plan(T, topo)["coll"], []
+    for r in ranks:
+        c = coll[r][which]
+        if c not in out and c != coll[source][which]:
+            out.append(c)
+    return out
+
+
+def part(topo, core, dests, sizes):
+    m = topo.mask(core, dests[0])
+    for d in dests:
+        m &= topo.mask(core, d)
+    bits = [1 << b for b in range(m.bit_length()) if m >> b & 1]
+    out, a = [], 0
+    for n in sizes:
+        out.append(sum(bits[a:a + n]))
+        a += n
+    return out
+
+
+def codes(ap):
+    return ap.bitcast(dt.uint8)
+
+
+def send(g, core, T, topo, parts, sent):
+    every = []
+    for p in parts:
+        every += p[3]
+    masks = part(topo, core, every, [ENGINES // len(parts)] * len(parts))
+    trs = []
+    for (kind, name, sem, dests), m in zip(parts, masks):
+        ids = []
+        for d in dests:
+            rid, pid = topo.addr(d, core)
+            ids.append(DstId(rid=rid, pnc=pid))
+        v = codes(T[kind + name][:]) if kind == "d" else T[kind + name][:]
+        trs.append(RemoteDMATransfer(dst_ids=ids, dma_engine_mask=m, remote_sem=T.sem[sem], srcs=[v], dsts=[v] * len(dests)))
+    g.remote_dma_fused(trs, local_sem=T.sem.sent)
+    sent[0] += ENGINES
+
+
+def k_part(l, s, dests):
+    return ("d", "%s%d" % (l, s), "k%s%d" % (l, s), dests)
+
+
+def p_part(l, s, dests):
+    return ("e", "%s%d" % (l, s), "p%s%d" % (l, s), dests)
+
+
+def plane_count(l, s):
+    return ENGINES // 2 if l != "A" and s < G else ENGINES
+
+
+def relay_program(g, core, T, topo, jobs):
+    sent = [0]
+    for s, it, ranks in jobs:
+        ds = [T.cores[r] for r in ranks]
+        late = [T.cores[r] for r in ranks if r not in EARLY.get(s, [])]
+        ck, cp = collectors(T, topo, s, ranks, 0), collectors(T, topo, s, ranks, 1)
+        if it == "T":
+            g.wait_ge(T.sem["kC%d" % s], ENGINES)
+            send(g, core, T, topo, [k_part("C", s, ck)], sent)
+            g.wait_ge(T.sem["pC%d" % s], plane_count("C", s))
+            send(g, core, T, topo, [p_part("C", s, cp)], sent)
+        elif it == "P":
+            g.wait_ge(T.sem["pA%d" % s], plane_count("A", s))
+            send(g, core, T, topo, [p_part("A", s, late)], sent)
+            g.wait_ge(T.sem["pB%d" % s], plane_count("B", s))
+            g.wait_ge(T.sem["pC%d" % s], plane_count("C", s))
+            send(g, core, T, topo, [p_part("B", s, ds), p_part("C", s, cp)], sent)
+        else:
+            g.wait_ge(T.sem["k%s%d" % (it, s)], ENGINES)
+            send(g, core, T, topo, [k_part(it, s, {"A": late, "B": ds, "C": ck}[it])], sent)
+    g.wait_ge(T.sem.sent, sent[0])
+
+
+def collector_program(g, core, T, topo, kind, ranks):
+    sent, ds = [0], [T.cores[r] for r in ranks]
+    for m in PAIRS:
+        for h in (0, 1):
+            s = 2 * m + h
+            q = g.sync if h == 0 else g.scalar
+            a, b = 128 * h, 128 * h + 128
+            if kind == "k":
+                q.wait_ge(T.sem["kC%d" % s], ENGINES)
+                q.dma_start(codes(T["dp%d" % m][:, a:b]), codes(T["dC%d" % s][:])).then_inc(T.sem["cb%d" % m], 16)
+            else:
+                q.wait_ge(T.sem["pC%d" % s], plane_count("C", s))
+                q.dma_start(T["ep%d" % m][:, a:b], T["eC%d" % s][:]).then_inc(T.sem["cb%d" % m], 16)
+        g.wait_ge(T.sem["cb%d" % m], 32)
+        send(g, core, T, topo, [("d" if kind == "k" else "e", "p%d" % m, ("kp%d" if kind == "k" else "pp%d") % m, ds)], sent)
+    g.wait_ge(T.sem.sent, sent[0])
+
+
+def rank_program(g, core, T, topo):
+    rank = T.rank_of(core)
+    pl = plan(T, topo)
+    if rank is None:
+        if core in pl["jobs"]:
+            relay_program(g, core, T, topo, pl["jobs"][core])
+        elif core in pl["serves"]:
+            collector_program(g, core, T, topo, *pl["serves"][core])
+        return
+    S = T.sem
+    sy, sc, ve, te = g.sync, g.scalar, g.vector, g.tensor
+    own = rank < G
+    inp = {"A": (T.ac, T.az), "B": (T.bc, T.bs), "C": (T.cc, T.cs)}
+    order = ORDER[rank]
+
+    def stage_codes(l):
+        sy.dma_start(codes(T["d%s%d" % (l, rank)][:]), inp[l][0][:]).then_inc(S["g" + l], 16)
+
+    def stage_plane(l):
+        sc.dma_start(T["e%s%d" % (l, rank)][:], inp[l][1][:]).then_inc(S.gpA if l == "A" else S.gpC, 16)
+
+    def fetch_codes(l, k):
+        i = order[k]
+        if i == rank:
+            src = inp[l][0][:]
+        else:
+            sy.wait_ge(S["k%s%d" % (l, i)], ENGINES)
+            src = codes(T["d%s%d" % (l, i)][:])
+        if k:
+            sy.wait_ge(S[("z%d" if l == "A" else "yy%d") % (k - 1)], 1)
+        sy.dma_start(codes(T["w" + l][:]), src).then_inc(S["f%s%d" % (l, k)], 16)
+
+    def plane_at(l, k):
+        return T["v" + l][:, 128 * (k % 2):128 * (k % 2) + 128]
+
+    def fetch_plane(l, k):
+        i = order[k]
+        if i == rank:
+            src = inp[l][1][:]
+        else:
+            sc.wait_ge(S["p%s%d" % (l, i)], plane_count(l, i))
+            src = T["e%s%d" % (l, i)][:]
+        if k >= 2:
+            sc.wait_ge(S[("z%d" if l == "A" else "yy%d") % (k - 2)], 1)
+        sc.dma_start(plane_at(l, k), src).then_inc(S["vf%s%d" % (l, k)], 16)
+
+    def fetch_pair(n):
+        m = PAIRS[n]
+        sy.wait_ge(S["kp%d" % m], ENGINES)
+        sy.wait_ge(S["pp%d" % m], ENGINES)
+        if n:
+            sy.wait_ge(S["mm%d" % (2 * n - 2)], 1)
+            sy.wait_ge(S["mm%d" % (2 * n - 1)], 1)
+        sy.dma_start(codes(T.wC[:]), codes(T["dp%d" % m][:])).then_inc(S["fC%d" % n], 16)
+        sy.dma_start(T.vC[:], T["ep%d" % m][:]).then_inc(S["fC%d" % n], 16)
+
+    def q_codes(q):
+        a = 128 * "xgh".index(q)
+        return T.qc[:, a:a + 128]
+
+    def q_scales(q):
+        a = 128 * "xgh".index(q)
+        return T.qs[:, a:a + 128]
+
+    if own:
+        stage_codes("A")
+        stage_plane("A")
+        fetch_codes("A", 0)
+    sc.dma_start(T.xt[:], T.x[:]).then_inc(S.lx, 16)
+    if own:
+        fetch_plane("A", 0)
+        stage_codes("B")
+        stage_plane("B")
+    stage_codes("C")
+    stage_plane("C")
+
+    sent, hop1, coll = [0], pl["hop1"], pl["coll"][rank]
+    if own:
+        early = [T.cores[r] for r in EARLY[rank]]
+        g.wait_ge(S.gA, 16)
+        send(g, core, T, topo, [k_part("A", rank, hop1[(rank, "A")])], sent)
+        g.wait_ge(S.gpA, 16)
+        send(g, core, T, topo, [p_part("A", rank, hop1[(rank, "P")] + early)], sent)
+        send(g, core, T, topo, [k_part("A", rank, early)], sent)
+        g.wait_ge(S.gB, 16)
+        send(g, core, T, topo, [k_part("B", rank, hop1[(rank, "B")])], sent)
+        g.wait_ge(S.gpC, 32)
+        send(g, core, T, topo, [p_part("B", rank, hop1[(rank, "P")]), p_part("C", rank, hop1[(rank, "P")] + [coll[1]])], sent)
+        g.wait_ge(S.gC, 16)
+        send(g, core, T, topo, [k_part("C", rank, hop1[(rank, "C")] + [coll[0]])], sent)
+    else:
+        g.wait_ge(S.gC, 16)
+        send(g, core, T, topo, [k_part("C", rank, hop1[(rank, "T")] + [coll[0]])], sent)
+        g.wait_ge(S.gpC, 16)
+        send(g, core, T, topo, [p_part("C", rank, hop1[(rank, "T")] + [coll[1]])], sent)
+    g.wait_ge(S.sent, sent[0])
+
+    for l in "AB":
+        for k in range(1 if own and l == "A" else 0, G):
+            fetch_codes(l, k)
+            fetch_plane(l, k)
+    fetch_pair(0)
+
+    ve.wait_ge(S.lx, 16)
+    ve.quantize_mx(q_codes("x"), q_scales("x"), T.xt[:]).then_inc(S.xq, 1)
+    for l, z, a, q, src, dst in (("A", "z", "ga", "gq", "x", "g"), ("B", "yy", "ha", "hq", "g", "h")):
+        te.wait_ge(S["xq" if l == "A" else "gq"], 1)
+        tile = T[dst + "t"]
+        for k in range(G):
+            bank = T["ps" + l][:, 512 * (k % 2):512 * (k % 2) + 128]
+            if k >= 2:
+                te.wait_ge(S[a + str(k - 2)], 1)
+            te.wait_ge(S["vf%s%d" % (l, k)], 16)
+            te.wait_ge(S["f%s%d" % (l, k)], 16)
+            te.matmul_mx(bank, T["w" + l][:], plane_at(l, k), q_codes(src), q_scales(src), True, True).then_inc(S[z + str(k)], 1)
+            ve.wait_ge(S[z + str(k)], 1)
+            ve.tensor_scalar(tile[:, order[k]:512:4], bank, 0.0, SCALE, AluOpType.max, AluOpType.mult).then_inc(S[a + str(k)], 1)
+        for k in range(G):
+            ve.wait_ge(S[a + str(k)], 1)
+        ve.quantize_mx(q_codes(dst), q_scales(dst), tile[:]).then_inc(S[q], 1)
+    te.wait_ge(S.hq, 1)
+
+    for n in range(N // 2):
+        m = PAIRS[n]
+        banks = [T.psC[:, 512 * (2 * (n % 2) + h):512 * (2 * (n % 2) + h) + 128] for h in (0, 1)]
+        te.wait_ge(S["fC%d" % n], 32)
+        for h in (0, 1):
+            if n >= 2:
+                te.wait_ge(S["cp%d" % (2 * n - 4 + h)], 1)
+            te.matmul_mx(banks[h], T.wC[:, 128 * h:128 * h + 128], T.vC[:, 128 * h:128 * h + 128], q_codes("h"), q_scales("h"), True,
+                         True).then_inc(S["mm%d" % (2 * n + h)], 1)
+        if n + 1 < N // 2:
+            fetch_pair(n + 1)
+        for h, e in ((0, sc), (1, ve)):
+            e.wait_ge(S["mm%d" % (2 * n + h)], 1)
+            if n:
+                e.wait_ge(S["st%d" % (n - 1)], 16)
+            blk = T.yb[:, 128 * h:128 * h + 128]
+            if e is sc:
+                sc.activation(blk, banks[h], ActivationFunctionType.Copy).then_inc(S["cp%d" % (2 * n)], 1)
+            else:
+                ve.tensor_copy(blk, banks[h]).then_inc(S["cp%d" % (2 * n + 1)], 1)
+        sc.wait_ge(S["cp%d" % (2 * n)], 1)
+        sc.wait_ge(S["cp%d" % (2 * n + 1)], 1)
+        sc.dma_start(T.y[:, 256 * m:256 * m + 256], T.yb[:]).then_inc(S["st%d" % n], 16)
+    sc.wait_ge(S["st%d" % (N // 2 - 1)], 16)

@@ -1,5 +1,5 @@
 from concourse.bass import DstId, RemoteDMATransfer
-from concourse.mybir import dt, AluOpType, ActivationFunctionType
+from concourse.mybir import dt, AluOpType
 
 N = 10
 G = 4
@@ -23,7 +23,7 @@ SCRATCH = {
     "psB": ("psum", [128, 1024], "float32"),
     "psC": ("psum", [128, 2048], "float32"),
 }
-SEMAPHORES = ["sent", "gA", "gB", "gC", "gpA", "gpC", "lx", "xq", "gq", "hq"]
+SEMAPHORES = ["sent", "gA", "gB", "gC", "gpA", "gpB", "gpC", "lx", "xq", "gq", "hq"]
 for _l, _n in (("A", G), ("B", G), ("C", N)):
     for _i in range(_n):
         SCRATCH["d%s%d" % (_l, _i)] = ("dram", [128, 128], "float8_e4m3fn_x4")
@@ -31,39 +31,40 @@ for _l, _n in (("A", G), ("B", G), ("C", N)):
         SEMAPHORES += ["k%s%d" % (_l, _i), "p%s%d" % (_l, _i)]
 for _i in range(G):
     SEMAPHORES += [_s + str(_i) for _s in ("z", "ga", "yy", "ha", "fA", "vfA", "fB", "vfB")]
-for _i in range(N // 2):
-    SCRATCH["dp%d" % _i] = ("dram", [128, 256], "float8_e4m3fn_x4")
-    SCRATCH["ep%d" % _i] = ("dram", [128, 256], "uint8")
-    SEMAPHORES += [_s + str(_i) for _s in ("cb", "kp", "pp", "fC", "st")]
 for _i in range(N):
-    SEMAPHORES += ["mm%d" % _i, "cp%d" % _i]
+    SEMAPHORES += [_s + str(_i) for _s in ("fC", "mm", "cp", "st")]
 
-ROUTES = [
-    (0, ("at", 2), [2, 8, 1, 3], {0: "AC", 1: "PB"}),
-    (0, ("at", 6), [6, 9, 4, 5, 7], {0: "AC", 1: "PB"}),
-    (2, ("at", 0), [0, 1, 3, 8, 6, 9], {0: "AC", 1: "PB"}),
-    (2, ("at", 4), [4, 5, 7], {0: "AC", 1: "PB"}),
-    (1, ("mate", 2), [2, 8, 3, 0], {0: "AC", 1: "PB"}),
-    (3, ("mate", 2), [2, 8, 1, 0], {3: "AC", 2: "PB"}),
-    (1, ("mate", 6), [6, 9, 7, 5, 4], {0: "A", 1: "P", 2: "C", 3: "B"}),
-    (3, ("at", 5), [5, 7, 4, 6, 9], {0: "A", 1: "P", 3: "BC"}),
-    (4, ("at", 6), [6, 5, 7], {2: "T"}),
-    (4, ("at", 2), [2, 0, 1, 3], {2: "T"}),
-    (6, ("at", 4), [4, 5, 7], {2: "T"}),
-    (6, ("at", 0), [0, 2, 1, 3], {2: "T"}),
-    (5, ("at", 7), [7, 4, 6], {0: "T"}),
-    (5, ("at", 3), [3, 1, 0, 2], {0: "T"}),
-    (7, ("at", 5), [5, 4, 6], {2: "T"}),
-    (7, ("at", 1), [1, 3, 0, 2], {0: "T"}),
-    (8, ("at", 0), [0, 1, 3, 6], {3: "T"}),
-    (8, ("at", 4), [4, 5, 7], {3: "T"}),
-    (9, ("at", 4), [4, 5, 7], {3: "T"}),
-    (9, ("at", 0), [0, 1, 3, 2], {3: "T"}),
-]
-EARLY = {0: [6, 9], 1: [7], 2: [4, 8], 3: [5]}
-ORDER = {0: [0, 2, 1, 3], 1: [1, 3, 0, 2], 2: [2, 0, 1, 3], 3: [3, 1, 0, 2], 8: [2, 0, 1, 3],
-         4: [2, 0, 1, 3], 5: [3, 2, 0, 1], 6: [0, 1, 2, 3], 9: [0, 1, 2, 3], 7: [1, 3, 0, 2]}
-PAIRS = [2, 3, 4, 0, 1]
+_SITE_02 = [["A0", "C4", "C0"], ["a0", "b0", "c4", "c0"], ["B0"]]
+_SITE_2 = [["A2", "C9", "C6"], ["a2", "c9", "b2", "c6", "c2"], ["B2"], ["C8", "c8", "C2"]]
+LANES = {
+    ("mate", 6): [["A1"], ["a1", "b1", "c1"], ["C1"], ["B1"]],
+    ("at", 5): [["A3", "C7"], ["a3", "b3", "c7", "c3"], ["B3"], ["C3"]],
+    ("at", 7): [["C5"], ["c5"]],
+    ("at", 6): _SITE_02,
+    ("at", 4): _SITE_2,
+    ("at", 2): _SITE_02,
+    ("at", 0): _SITE_2,
+    ("mate", 2): [["A1", "B3"], ["a1", "b1", "c1", "C1"], ["a3", "b3", "c3", "C3"], ["A3", "B1"]],
+    ("at", 3): [["C5"], ["c5"]],
+    ("at", 1): [["C7"], ["c7"]],
+}
+DESTS = {
+    ("at", 2): {0: [2, 8, 1, 3], 4: [2, 0, 1, 3]},
+    ("at", 6): {0: [6, 9, 4, 5, 7], 4: [6, 5, 7]},
+    ("at", 0): {2: [6, 9, 0, 1, 3], 6: [0, 2, 1, 3], 8: [0, 1, 3, 6], 9: [0, 1, 3, 2]},
+    ("at", 4): {2: [4, 5, 7], 6: [4, 5, 7], 8: [4, 5, 7], 9: [4, 5, 7]},
+    ("mate", 2): {1: [2, 8, 3, 0], 3: [2, 8, 1, 0]},
+    ("mate", 6): {1: [6, 9, 7, 5, 4]},
+    ("at", 5): {3: [5, 7, 4, 6, 9], 7: [5, 4, 6]},
+    ("at", 7): {5: [7, 4, 6]},
+    ("at", 3): {5: [3, 1, 0, 2]},
+    ("at", 1): {7: [1, 3, 0, 2]},
+}
+EARLY = {0: [6, 9, 2], 1: [7, 3], 2: [4, 8, 0], 3: [5, 1]}
+FIRST = {(("at", 6), 0): [4], (("mate", 6), 1): [6, 9], (("at", 4), 2): [5], (("at", 5), 3): [7]}
+ORDER = {0: [0, 2, 1, 3], 1: [1, 3, 0, 2], 2: [2, 0, 3, 1], 3: [3, 1, 2, 0], 8: [2, 0, 1, 3],
+         4: [2, 0, 3, 1], 5: [3, 2, 0, 1], 6: [0, 1, 2, 3], 9: [0, 1, 2, 3], 7: [1, 3, 0, 2]}
+C_ORDER = [9, 5, 7, 6, 8, 4, 2, 1, 0, 3]
 ENGINES = 8
 _PLAN = {}
 
@@ -81,129 +82,108 @@ def site_cores(T, topo, site, served):
     far = [c for c in cs if topo.die(c) != topo.die(ref)]
     out = []
     for i in range(max(len(near), len(far))):
-        out += near[i:i + 1] + far[i:i + 1]
+        out += far[i:i + 1] + near[i:i + 1]
     return out
 
 
 def plan(T, topo):
     if _PLAN:
         return _PLAN
-    hop1, jobs, coll, serves = {}, {}, {}, {}
-    for s, site, dests, lanes in ROUTES:
+    hop1, jobs, coll, serves, here, fan, fans = {}, {}, {}, {}, {}, {}, {}
+    for site, lanes in LANES.items():
         served = set()
-        for r in ROUTES:
-            if r[1] == site:
-                served.update(r[2])
+        for ds in DESTS[site].values():
+            served.update(ds)
         cs = site_cores(T, topo, site, served)
-        for n, items in lanes.items():
-            for it in items:
-                hop1.setdefault((s, it), []).append(cs[n])
-                jobs.setdefault(cs[n], []).append((s, it, dests))
+        for core, items in zip(cs, lanes):
+            for item in items:
+                l, s = item[0], int(item[1:])
+                ds, first = DESTS[site][s], []
+                if l in "Aa":
+                    first = FIRST.get((site, s), [])
+                    ds = [r for r in ds if r not in EARLY[s]]
+                groups = [first, [r for r in ds if r not in first]]
+                hop1.setdefault(item, []).append(core)
+                jobs.setdefault(core, []).append((l, s, [x for x in groups if x]))
     for r in range(N):
-        here = [q for q in range(N) if same_chip(topo, T.cores[q], T.cores[r])]
-        free = [c for c in site_cores(T, topo, ("at", r), here) if c not in jobs]
-        coll[r] = (free[0], free[1])
-        serves[free[0]] = ("k", here)
-        serves[free[1]] = ("p", here)
-    _PLAN["hop1"] = hop1
-    _PLAN["jobs"] = jobs
-    _PLAN["coll"] = coll
-    _PLAN["serves"] = serves
+        here[r] = [q for q in range(N) if same_chip(topo, T.cores[q], T.cores[r])]
+        free = [c for c in site_cores(T, topo, ("at", r), here[r]) if c not in jobs]
+        if len(here[r]) > 1:
+            coll[r] = (free[0], free[1])
+            serves[free[0]] = (0, here[r])
+            serves[free[1]] = (1, here[r])
+        if r < G:
+            fan[r] = free[2]
+            fans[free[2]] = r
+    for k, v in (("hop1", hop1), ("jobs", jobs), ("coll", coll), ("serves", serves), ("here", here), ("fan", fan), ("fans", fans)):
+        _PLAN[k] = v
     return _PLAN
-
-
-def collectors(T, topo, source, ranks, which):
-    coll, out = plan(T, topo)["coll"], []
-    for r in ranks:
-        c = coll[r][which]
-        if c not in out and c != coll[source][which]:
-            out.append(c)
-    return out
-
-
-def part(topo, core, dests, sizes):
-    m = topo.mask(core, dests[0])
-    for d in dests:
-        m &= topo.mask(core, d)
-    bits = [1 << b for b in range(m.bit_length()) if m >> b & 1]
-    out, a = [], 0
-    for n in sizes:
-        out.append(sum(bits[a:a + n]))
-        a += n
-    return out
 
 
 def codes(ap):
     return ap.bitcast(dt.uint8)
 
 
-def send(g, core, T, topo, parts, sent):
-    every = []
-    for p in parts:
-        every += p[3]
-    masks = part(topo, core, every, [ENGINES // len(parts)] * len(parts))
-    trs = []
-    for (kind, name, sem, dests), m in zip(parts, masks):
-        ids = []
-        for d in dests:
-            rid, pid = topo.addr(d, core)
-            ids.append(DstId(rid=rid, pnc=pid))
-        v = codes(T[kind + name][:]) if kind == "d" else T[kind + name][:]
-        trs.append(RemoteDMATransfer(dst_ids=ids, dma_engine_mask=m, remote_sem=T.sem[sem], srcs=[v], dsts=[v] * len(dests)))
-    g.remote_dma_fused(trs, local_sem=T.sem.sent)
-    sent[0] += ENGINES
+def tile_of(T, l, s):
+    return codes(T["d%s%d" % (l, s)][:]) if l in "ABC" else T["e%s%d" % (l.upper(), s)][:]
 
 
-def k_part(l, s, dests):
-    return ("d", "%s%d" % (l, s), "k%s%d" % (l, s), dests)
+def sem_of(T, l, s):
+    return T.sem["k%s%d" % (l, s)] if l in "ABC" else T.sem["p%s%d" % (l.upper(), s)]
 
 
-def p_part(l, s, dests):
-    return ("e", "%s%d" % (l, s), "p%s%d" % (l, s), dests)
+def send(g, core, T, topo, l, s, dests, sent, wide=False):
+    m = topo.mask(core, dests[0])
+    for d in dests:
+        m &= topo.mask(core, d)
+    bits = [1 << b for b in range(m.bit_length()) if m >> b & 1]
+    bits = bits if wide else bits[:ENGINES]
+    ids = []
+    for d in dests:
+        rid, pid = topo.addr(d, core)
+        ids.append(DstId(rid=rid, pnc=pid))
+    v = tile_of(T, l, s)
+    tr = RemoteDMATransfer(dst_ids=ids, dma_engine_mask=sum(bits), remote_sem=sem_of(T, l, s), srcs=[v], dsts=[v] * len(ids))
+    g.remote_dma_fused([tr], local_sem=T.sem.sent)
+    sent[0] += len(bits)
 
 
-def plane_count(l, s):
-    return ENGINES // 2 if l != "A" and s < G else ENGINES
+def c_dests(T, topo, l, source, ranks):
+    pl, out = plan(T, topo), []
+    for r in ranks:
+        if r in pl["here"][source]:
+            continue
+        c = pl["coll"][r]["Cc".index(l)] if r in pl["coll"] else T.cores[r]
+        if c not in out:
+            out.append(c)
+    return out
 
 
 def relay_program(g, core, T, topo, jobs):
     sent = [0]
-    for s, it, ranks in jobs:
-        ds = [T.cores[r] for r in ranks]
-        late = [T.cores[r] for r in ranks if r not in EARLY.get(s, [])]
-        ck, cp = collectors(T, topo, s, ranks, 0), collectors(T, topo, s, ranks, 1)
-        if it == "T":
-            g.wait_ge(T.sem["kC%d" % s], ENGINES)
-            send(g, core, T, topo, [k_part("C", s, ck)], sent)
-            g.wait_ge(T.sem["pC%d" % s], plane_count("C", s))
-            send(g, core, T, topo, [p_part("C", s, cp)], sent)
-        elif it == "P":
-            g.wait_ge(T.sem["pA%d" % s], plane_count("A", s))
-            send(g, core, T, topo, [p_part("A", s, late)], sent)
-            g.wait_ge(T.sem["pB%d" % s], plane_count("B", s))
-            g.wait_ge(T.sem["pC%d" % s], plane_count("C", s))
-            send(g, core, T, topo, [p_part("B", s, ds), p_part("C", s, cp)], sent)
-        else:
-            g.wait_ge(T.sem["k%s%d" % (it, s)], ENGINES)
-            send(g, core, T, topo, [k_part(it, s, {"A": late, "B": ds, "C": ck}[it])], sent)
+    for l, s, groups in jobs:
+        g.wait_ge(sem_of(T, l, s), ENGINES)
+        for ranks in groups:
+            ds = c_dests(T, topo, l, s, ranks) if l in "Cc" else [T.cores[r] for r in ranks]
+            send(g, core, T, topo, l, s, ds, sent)
     g.wait_ge(T.sem.sent, sent[0])
 
 
-def collector_program(g, core, T, topo, kind, ranks):
-    sent, ds = [0], [T.cores[r] for r in ranks]
-    for m in PAIRS:
-        for h in (0, 1):
-            s = 2 * m + h
-            q = g.sync if h == 0 else g.scalar
-            a, b = 128 * h, 128 * h + 128
-            if kind == "k":
-                q.wait_ge(T.sem["kC%d" % s], ENGINES)
-                q.dma_start(codes(T["dp%d" % m][:, a:b]), codes(T["dC%d" % s][:])).then_inc(T.sem["cb%d" % m], 16)
-            else:
-                q.wait_ge(T.sem["pC%d" % s], plane_count("C", s))
-                q.dma_start(T["ep%d" % m][:, a:b], T["eC%d" % s][:]).then_inc(T.sem["cb%d" % m], 16)
-        g.wait_ge(T.sem["cb%d" % m], 32)
-        send(g, core, T, topo, [("d" if kind == "k" else "e", "p%d" % m, ("kp%d" if kind == "k" else "pp%d") % m, ds)], sent)
+def fan_program(g, core, T, topo, s):
+    pl, sent = plan(T, topo), [0]
+    twin = [T.cores[r] for r in pl["here"][s] if r != s]
+    for l in "Cc":
+        g.wait_ge(sem_of(T, l, s), ENGINES)
+        send(g, core, T, topo, l, s, pl["hop1"]["%s%d" % (l, s)] + twin, sent)
+    g.wait_ge(T.sem.sent, sent[0])
+
+
+def collector_program(g, core, T, topo, which, ranks):
+    sent, ds, l = [0], [T.cores[r] for r in ranks], "Cc"[which]
+    for s in C_ORDER:
+        if s not in ranks:
+            g.wait_ge(sem_of(T, l, s), ENGINES)
+            send(g, core, T, topo, l, s, ds, sent, wide=True)
     g.wait_ge(T.sem.sent, sent[0])
 
 
@@ -215,26 +195,34 @@ def rank_program(g, core, T, topo):
             relay_program(g, core, T, topo, pl["jobs"][core])
         elif core in pl["serves"]:
             collector_program(g, core, T, topo, *pl["serves"][core])
+        elif core in pl["fans"]:
+            fan_program(g, core, T, topo, pl["fans"][core])
         return
     S = T.sem
     sy, sc, ve, te = g.sync, g.scalar, g.vector, g.tensor
     own = rank < G
     inp = {"A": (T.ac, T.az), "B": (T.bc, T.bs), "C": (T.cc, T.cs)}
     order = ORDER[rank]
+    here = pl["here"][rank]
+    c_order = [rank] + [s for s in here if s != rank] + [s for s in C_ORDER if s not in here]
+    wide_count = ENGINES
+    if rank in pl["coll"]:
+        m = topo.mask(pl["coll"][rank][0], core)
+        wide_count = len([b for b in range(m.bit_length()) if m >> b & 1])
 
     def stage_codes(l):
-        sy.dma_start(codes(T["d%s%d" % (l, rank)][:]), inp[l][0][:]).then_inc(S["g" + l], 16)
+        sy.dma_start(tile_of(T, l, rank), inp[l][0][:]).then_inc(S["g" + l], 16)
 
     def stage_plane(l):
-        sc.dma_start(T["e%s%d" % (l, rank)][:], inp[l][1][:]).then_inc(S.gpA if l == "A" else S.gpC, 16)
+        sc.dma_start(tile_of(T, l.lower(), rank), inp[l][1][:]).then_inc(S["gp" + l], 16)
 
     def fetch_codes(l, k):
         i = order[k]
         if i == rank:
             src = inp[l][0][:]
         else:
-            sy.wait_ge(S["k%s%d" % (l, i)], ENGINES)
-            src = codes(T["d%s%d" % (l, i)][:])
+            sy.wait_ge(sem_of(T, l, i), ENGINES)
+            src = tile_of(T, l, i)
         if k:
             sy.wait_ge(S[("z%d" if l == "A" else "yy%d") % (k - 1)], 1)
         sy.dma_start(codes(T["w" + l][:]), src).then_inc(S["f%s%d" % (l, k)], 16)
@@ -247,21 +235,25 @@ def rank_program(g, core, T, topo):
         if i == rank:
             src = inp[l][1][:]
         else:
-            sc.wait_ge(S["p%s%d" % (l, i)], plane_count(l, i))
-            src = T["e%s%d" % (l, i)][:]
+            sc.wait_ge(sem_of(T, l.lower(), i), ENGINES)
+            src = tile_of(T, l.lower(), i)
         if k >= 2:
             sc.wait_ge(S[("z%d" if l == "A" else "yy%d") % (k - 2)], 1)
         sc.dma_start(plane_at(l, k), src).then_inc(S["vf%s%d" % (l, k)], 16)
 
-    def fetch_pair(n):
-        m = PAIRS[n]
-        sy.wait_ge(S["kp%d" % m], ENGINES)
-        sy.wait_ge(S["pp%d" % m], ENGINES)
-        if n:
-            sy.wait_ge(S["mm%d" % (2 * n - 2)], 1)
-            sy.wait_ge(S["mm%d" % (2 * n - 1)], 1)
-        sy.dma_start(codes(T.wC[:]), codes(T["dp%d" % m][:])).then_inc(S["fC%d" % n], 16)
-        sy.dma_start(T.vC[:], T["ep%d" % m][:]).then_inc(S["fC%d" % n], 16)
+    def fetch_c(j):
+        i = c_order[j]
+        if i == rank:
+            kc, pc = T.cc[:], T.cs[:]
+        else:
+            n = ENGINES if i in here else wide_count
+            sy.wait_ge(sem_of(T, "C", i), n)
+            sy.wait_ge(sem_of(T, "c", i), n)
+            kc, pc = tile_of(T, "C", i), tile_of(T, "c", i)
+        if j >= 2:
+            sy.wait_ge(S["mm%d" % (j - 2)], 1)
+        sy.dma_start(codes(T.wC[:, 128 * (j % 2):128 * (j % 2) + 128]), kc).then_inc(S["fC%d" % j], 16)
+        sy.dma_start(plane_at("C", j), pc).then_inc(S["fC%d" % j], 16)
 
     def q_codes(q):
         a = 128 * "xgh".index(q)
@@ -282,33 +274,36 @@ def rank_program(g, core, T, topo):
         stage_plane("B")
     stage_codes("C")
     stage_plane("C")
+    if own:
+        fetch_codes("B", 0)
+        fetch_plane("B", 0)
+    fetch_c(0)
 
-    sent, hop1, coll = [0], pl["hop1"], pl["coll"][rank]
+    sent, hop1 = [0], pl["hop1"]
+    twin = [T.cores[r] for r in here if r != rank]
+    c_to = {l: [pl["fan"][rank]] if own else hop1["%s%d" % (l, rank)] + twin for l in "Cc"}
     if own:
         early = [T.cores[r] for r in EARLY[rank]]
         g.wait_ge(S.gA, 16)
-        send(g, core, T, topo, [k_part("A", rank, hop1[(rank, "A")])], sent)
+        send(g, core, T, topo, "A", rank, hop1["A%d" % rank], sent)
         g.wait_ge(S.gpA, 16)
-        send(g, core, T, topo, [p_part("A", rank, hop1[(rank, "P")] + early)], sent)
-        send(g, core, T, topo, [k_part("A", rank, early)], sent)
+        send(g, core, T, topo, "a", rank, hop1["a%d" % rank] + early, sent)
+        send(g, core, T, topo, "A", rank, early, sent)
         g.wait_ge(S.gB, 16)
-        send(g, core, T, topo, [k_part("B", rank, hop1[(rank, "B")])], sent)
-        g.wait_ge(S.gpC, 32)
-        send(g, core, T, topo, [p_part("B", rank, hop1[(rank, "P")]), p_part("C", rank, hop1[(rank, "P")] + [coll[1]])], sent)
-        g.wait_ge(S.gC, 16)
-        send(g, core, T, topo, [k_part("C", rank, hop1[(rank, "C")] + [coll[0]])], sent)
-    else:
-        g.wait_ge(S.gC, 16)
-        send(g, core, T, topo, [k_part("C", rank, hop1[(rank, "T")] + [coll[0]])], sent)
-        g.wait_ge(S.gpC, 16)
-        send(g, core, T, topo, [p_part("C", rank, hop1[(rank, "T")] + [coll[1]])], sent)
+        send(g, core, T, topo, "B", rank, hop1["B%d" % rank] + twin, sent)
+        g.wait_ge(S.gpB, 16)
+        send(g, core, T, topo, "b", rank, hop1["b%d" % rank] + twin, sent)
+    g.wait_ge(S.gC, 16)
+    send(g, core, T, topo, "C", rank, c_to["C"], sent, wide=False)
+    g.wait_ge(S.gpC, 16)
+    send(g, core, T, topo, "c", rank, c_to["c"], sent, wide=False)
     g.wait_ge(S.sent, sent[0])
 
     for l in "AB":
-        for k in range(1 if own and l == "A" else 0, G):
+        for k in range(1 if own else 0, G):
             fetch_codes(l, k)
             fetch_plane(l, k)
-    fetch_pair(0)
+    fetch_c(1)
 
     ve.wait_ge(S.lx, 16)
     ve.quantize_mx(q_codes("x"), q_scales("x"), T.xt[:]).then_inc(S.xq, 1)
@@ -329,27 +324,22 @@ def rank_program(g, core, T, topo):
         ve.quantize_mx(q_codes(dst), q_scales(dst), tile[:]).then_inc(S[q], 1)
     te.wait_ge(S.hq, 1)
 
-    for n in range(N // 2):
-        m = PAIRS[n]
-        banks = [T.psC[:, 512 * (2 * (n % 2) + h):512 * (2 * (n % 2) + h) + 128] for h in (0, 1)]
-        te.wait_ge(S["fC%d" % n], 32)
-        for h in (0, 1):
-            if n >= 2:
-                te.wait_ge(S["cp%d" % (2 * n - 4 + h)], 1)
-            te.matmul_mx(banks[h], T.wC[:, 128 * h:128 * h + 128], T.vC[:, 128 * h:128 * h + 128], q_codes("h"), q_scales("h"), True,
-                         True).then_inc(S["mm%d" % (2 * n + h)], 1)
-        if n + 1 < N // 2:
-            fetch_pair(n + 1)
-        for h, e in ((0, sc), (1, ve)):
-            e.wait_ge(S["mm%d" % (2 * n + h)], 1)
-            if n:
-                e.wait_ge(S["st%d" % (n - 1)], 16)
-            blk = T.yb[:, 128 * h:128 * h + 128]
-            if e is sc:
-                sc.activation(blk, banks[h], ActivationFunctionType.Copy).then_inc(S["cp%d" % (2 * n)], 1)
-            else:
-                ve.tensor_copy(blk, banks[h]).then_inc(S["cp%d" % (2 * n + 1)], 1)
-        sc.wait_ge(S["cp%d" % (2 * n)], 1)
-        sc.wait_ge(S["cp%d" % (2 * n + 1)], 1)
-        sc.dma_start(T.y[:, 256 * m:256 * m + 256], T.yb[:]).then_inc(S["st%d" % n], 16)
-    sc.wait_ge(S["st%d" % (N // 2 - 1)], 16)
+    for j in range(N):
+        bank = T.psC[:, 512 * (j % 4):512 * (j % 4) + 128]
+        blk = T.yb[:, 128 * (j % 2):128 * (j % 2) + 128]
+        i = c_order[j]
+        te.wait_ge(S["fC%d" % j], 32)
+        if j >= 4:
+            te.wait_ge(S["cp%d" % (j - 4)], 1)
+        te.matmul_mx(bank, T.wC[:, 128 * (j % 2):128 * (j % 2) + 128], plane_at("C", j), q_codes("h"), q_scales("h"), True,
+                     True).then_inc(S["mm%d" % j], 1)
+        if j + 2 < N:
+            fetch_c(j + 2)
+        ve.wait_ge(S["mm%d" % j], 1)
+        if j >= 2:
+            ve.wait_ge(S["st%d" % (j - 2)], 16)
+        ve.tensor_copy(blk, bank).then_inc(S["cp%d" % j], 1)
+        sc.wait_ge(S["cp%d" % j], 1)
+        sc.dma_start(T.y[:, 128 * i:128 * i + 128], blk).then_inc(S["st%d" % j], 16)
+    sc.wait_ge(S["st%d" % (N - 2)], 16)
+    sc.wait_ge(S["st%d" % (N - 1)], 16)

from concourse.bass import DstId, RemoteDMATransfer
from concourse.mybir import dt, AluOpType

N = 10
G = 4
SCALE = 0.037
SIM_CORES = 512

SCRATCH = {
    "xt": ("sbuf", [128, 512], "bfloat16"),
    "gt": ("sbuf", [128, 512], "bfloat16"),
    "ht": ("sbuf", [128, 512], "bfloat16"),
    "wA": ("sbuf", [128, 128], "float8_e4m3fn_x4"),
    "vA": ("sbuf", [128, 256], "uint8"),
    "wB": ("sbuf", [128, 128], "float8_e4m3fn_x4"),
    "vB": ("sbuf", [128, 256], "uint8"),
    "wC": ("sbuf", [128, 256], "float8_e4m3fn_x4"),
    "vC": ("sbuf", [128, 256], "uint8"),
    "yb": ("sbuf", [128, 256], "float32"),
    "qc": ("sbuf", [128, 384], "float8_e4m3fn_x4"),
    "qs": ("sbuf", [128, 384], "uint8"),
    "psA": ("psum", [128, 1024], "float32"),
    "psB": ("psum", [128, 1024], "float32"),
    "psC": ("psum", [128, 2048], "float32"),
}
SEMAPHORES = ["sent", "gA", "gB", "gC", "gpA", "gpB", "gpC", "lx", "xq", "gq", "hq"]
for _l, _n in (("A", G), ("B", G), ("C", N)):
    for _i in range(_n):
        SCRATCH["d%s%d" % (_l, _i)] = ("dram", [128, 128], "float8_e4m3fn_x4")
        SCRATCH["e%s%d" % (_l, _i)] = ("dram", [128, 128], "uint8")
        SEMAPHORES += ["k%s%d" % (_l, _i), "p%s%d" % (_l, _i)]
for _i in range(G):
    SEMAPHORES += [_s + str(_i) for _s in ("z", "ga", "yy", "ha", "fA", "vfA", "fB", "vfB")]
for _i in range(N):
    SEMAPHORES += [_s + str(_i) for _s in ("fC", "mm", "cp", "st")]

_SITE_02 = [["A0", "C4", "C0"], ["a0", "b0", "c4", "c0"], ["B0"]]
_SITE_2 = [["A2", "C9", "C6"], ["a2", "c9", "b2", "c6", "c2"], ["B2"], ["C8", "c8", "C2"]]
LANES = {
    ("mate", 6): [["A1"], ["a1", "b1", "c1"], ["C1"], ["B1"]],
    ("at", 5): [["A3", "C7"], ["a3", "b3", "c7", "c3"], ["B3"], ["C3"]],
    ("at", 7): [["C5"], ["c5"]],
    ("at", 6): _SITE_02,
    ("at", 4): _SITE_2,
    ("at", 2): _SITE_02,
    ("at", 0): _SITE_2,
    ("mate", 2): [["A1", "B3"], ["a1", "b1", "c1", "C1"], ["a3", "b3", "c3", "C3"], ["A3", "B1"]],
    ("at", 3): [["C5"], ["c5"]],
    ("at", 1): [["C7"], ["c7"]],
}
DESTS = {
    ("at", 2): {0: [2, 8, 1, 3], 4: [2, 0, 1, 3]},
    ("at", 6): {0: [6, 9, 4, 5, 7], 4: [6, 5, 7]},
    ("at", 0): {2: [6, 9, 0, 1, 3], 6: [0, 2, 1, 3], 8: [0, 1, 3, 6], 9: [0, 1, 3, 2]},
    ("at", 4): {2: [4, 5, 7], 6: [4, 5, 7], 8: [4, 5, 7], 9: [4, 5, 7]},
    ("mate", 2): {1: [2, 8, 3, 0], 3: [2, 8, 1, 0]},
    ("mate", 6): {1: [6, 9, 7, 5, 4]},
    ("at", 5): {3: [5, 7, 4, 6, 9], 7: [5, 4, 6]},
    ("at", 7): {5: [7, 4, 6]},
    ("at", 3): {5: [3, 1, 0, 2]},
    ("at", 1): {7: [1, 3, 0, 2]},
}
EARLY = {0: [6, 9, 2], 1: [7, 3], 2: [4, 8, 0], 3: [5, 1]}
FIRST = {(("at", 6), 0): [4], (("mate", 6), 1): [6, 9], (("at", 4), 2): [5], (("at", 5), 3): [7]}
ORDER = {0: [0, 2, 1, 3], 1: [1, 3, 0, 2], 2: [2, 0, 3, 1], 3: [3, 1, 2, 0], 8: [2, 0, 1, 3],
         4: [2, 0, 3, 1], 5: [3, 2, 0, 1], 6: [0, 1, 2, 3], 9: [0, 1, 2, 3], 7: [1, 3, 0, 2]}
C_ORDER = [9, 5, 7, 6, 8, 4, 2, 1, 0, 3]
ENGINES = 8
_PLAN = {}


def same_chip(topo, a, b):
    return topo.host(a) == topo.host(b) and topo.chip(a) == topo.chip(b)


def site_cores(T, topo, site, served):
    kind, r = site
    ref = T.cores[r]
    cs = [c for c in range(SIM_CORES) if (same_chip(topo, c, ref) if kind == "at" else topo.mates(c, ref))]
    cs = [c for c in cs if T.rank_of(c) is None and all(topo.may_write(c, T.cores[d]) for d in served)]
    near = [c for c in cs if topo.die(c) == topo.die(ref)]
    far = [c for c in cs if topo.die(c) != topo.die(ref)]
    out = []
    for i in range(max(len(near), len(far))):
        out += far[i:i + 1] + near[i:i + 1]
    return out


def plan(T, topo):
    if _PLAN:
        return _PLAN
    hop1, jobs, coll, serves, here, fan, fans = {}, {}, {}, {}, {}, {}, {}
    for site, lanes in LANES.items():
        served = set()
        for ds in DESTS[site].values():
            served.update(ds)
        cs = site_cores(T, topo, site, served)
        for core, items in zip(cs, lanes):
            for item in items:
                l, s = item[0], int(item[1:])
                ds, first = DESTS[site][s], []
                if l in "Aa":
                    first = FIRST.get((site, s), [])
                    ds = [r for r in ds if r not in EARLY[s]]
                groups = [first, [r for r in ds if r not in first]]
                hop1.setdefault(item, []).append(core)
                jobs.setdefault(core, []).append((l, s, [x for x in groups if x]))
    for r in range(N):
        here[r] = [q for q in range(N) if same_chip(topo, T.cores[q], T.cores[r])]
        free = [c for c in site_cores(T, topo, ("at", r), here[r]) if c not in jobs]
        if len(here[r]) > 1:
            coll[r] = (free[0], free[1])
            serves[free[0]] = (0, here[r])
            serves[free[1]] = (1, here[r])
        if r < G:
            fan[r] = free[2]
            fans[free[2]] = r
    for k, v in (("hop1", hop1), ("jobs", jobs), ("coll", coll), ("serves", serves), ("here", here), ("fan", fan), ("fans", fans)):
        _PLAN[k] = v
    return _PLAN


def codes(ap):
    return ap.bitcast(dt.uint8)


def tile_of(T, l, s):
    return codes(T["d%s%d" % (l, s)][:]) if l in "ABC" else T["e%s%d" % (l.upper(), s)][:]


def sem_of(T, l, s):
    return T.sem["k%s%d" % (l, s)] if l in "ABC" else T.sem["p%s%d" % (l.upper(), s)]


def send(g, core, T, topo, l, s, dests, sent, wide=False):
    m = topo.mask(core, dests[0])
    for d in dests:
        m &= topo.mask(core, d)
    bits = [1 << b for b in range(m.bit_length()) if m >> b & 1]
    bits = bits if wide else bits[:ENGINES]
    ids = []
    for d in dests:
        rid, pid = topo.addr(d, core)
        ids.append(DstId(rid=rid, pnc=pid))
    v = tile_of(T, l, s)
    tr = RemoteDMATransfer(dst_ids=ids, dma_engine_mask=sum(bits), remote_sem=sem_of(T, l, s), srcs=[v], dsts=[v] * len(ids))
    g.remote_dma_fused([tr], local_sem=T.sem.sent)
    sent[0] += len(bits)


def c_dests(T, topo, l, source, ranks):
    pl, out = plan(T, topo), []
    for r in ranks:
        if r in pl["here"][source]:
            continue
        c = pl["coll"][r]["Cc".index(l)] if r in pl["coll"] else T.cores[r]
        if c not in out:
            out.append(c)
    return out


def relay_program(g, core, T, topo, jobs):
    sent = [0]
    for l, s, groups in jobs:
        g.wait_ge(sem_of(T, l, s), ENGINES)
        for ranks in groups:
            ds = c_dests(T, topo, l, s, ranks) if l in "Cc" else [T.cores[r] for r in ranks]
            send(g, core, T, topo, l, s, ds, sent)
    g.wait_ge(T.sem.sent, sent[0])


def fan_program(g, core, T, topo, s):
    pl, sent = plan(T, topo), [0]
    twin = [T.cores[r] for r in pl["here"][s] if r != s]
    for l in "Cc":
        g.wait_ge(sem_of(T, l, s), ENGINES)
        send(g, core, T, topo, l, s, pl["hop1"]["%s%d" % (l, s)] + twin, sent)
    g.wait_ge(T.sem.sent, sent[0])


def collector_program(g, core, T, topo, which, ranks):
    sent, ds, l = [0], [T.cores[r] for r in ranks], "Cc"[which]
    for s in C_ORDER:
        if s not in ranks:
            g.wait_ge(sem_of(T, l, s), ENGINES)
            send(g, core, T, topo, l, s, ds, sent, wide=True)
    g.wait_ge(T.sem.sent, sent[0])


def rank_program(g, core, T, topo):
    rank = T.rank_of(core)
    pl = plan(T, topo)
    if rank is None:
        if core in pl["jobs"]:
            relay_program(g, core, T, topo, pl["jobs"][core])
        elif core in pl["serves"]:
            collector_program(g, core, T, topo, *pl["serves"][core])
        elif core in pl["fans"]:
            fan_program(g, core, T, topo, pl["fans"][core])
        return
    S = T.sem
    sy, sc, ve, te = g.sync, g.scalar, g.vector, g.tensor
    own = rank < G
    inp = {"A": (T.ac, T.az), "B": (T.bc, T.bs), "C": (T.cc, T.cs)}
    order = ORDER[rank]
    here = pl["here"][rank]
    c_order = [rank] + [s for s in here if s != rank] + [s for s in C_ORDER if s not in here]
    wide_count = ENGINES
    if rank in pl["coll"]:
        m = topo.mask(pl["coll"][rank][0], core)
        wide_count = len([b for b in range(m.bit_length()) if m >> b & 1])

    def stage_codes(l):
        sy.dma_start(tile_of(T, l, rank), inp[l][0][:]).then_inc(S["g" + l], 16)

    def stage_plane(l):
        sc.dma_start(tile_of(T, l.lower(), rank), inp[l][1][:]).then_inc(S["gp" + l], 16)

    def fetch_codes(l, k):
        i = order[k]
        if i == rank:
            src = inp[l][0][:]
        else:
            sy.wait_ge(sem_of(T, l, i), ENGINES)
            src = tile_of(T, l, i)
        if k:
            sy.wait_ge(S[("z%d" if l == "A" else "yy%d") % (k - 1)], 1)
        sy.dma_start(codes(T["w" + l][:]), src).then_inc(S["f%s%d" % (l, k)], 16)

    def plane_at(l, k):
        return T["v" + l][:, 128 * (k % 2):128 * (k % 2) + 128]

    def fetch_plane(l, k):
        i = order[k]
        if i == rank:
            src = inp[l][1][:]
        else:
            sc.wait_ge(sem_of(T, l.lower(), i), ENGINES)
            src = tile_of(T, l.lower(), i)
        if k >= 2:
            sc.wait_ge(S[("z%d" if l == "A" else "yy%d") % (k - 2)], 1)
        sc.dma_start(plane_at(l, k), src).then_inc(S["vf%s%d" % (l, k)], 16)

    def fetch_c(j):
        i = c_order[j]
        if i == rank:
            kc, pc = T.cc[:], T.cs[:]
        else:
            n = ENGINES if i in here else wide_count
            sy.wait_ge(sem_of(T, "C", i), n)
            sy.wait_ge(sem_of(T, "c", i), n)
            kc, pc = tile_of(T, "C", i), tile_of(T, "c", i)
        if j >= 2:
            sy.wait_ge(S["mm%d" % (j - 2)], 1)
        sy.dma_start(codes(T.wC[:, 128 * (j % 2):128 * (j % 2) + 128]), kc).then_inc(S["fC%d" % j], 16)
        sy.dma_start(plane_at("C", j), pc).then_inc(S["fC%d" % j], 16)

    def q_codes(q):
        a = 128 * "xgh".index(q)
        return T.qc[:, a:a + 128]

    def q_scales(q):
        a = 128 * "xgh".index(q)
        return T.qs[:, a:a + 128]

    if own:
        stage_codes("A")
        stage_plane("A")
        fetch_codes("A", 0)
    sc.dma_start(T.xt[:], T.x[:]).then_inc(S.lx, 16)
    if own:
        fetch_plane("A", 0)
        stage_codes("B")
        stage_plane("B")
    stage_codes("C")
    stage_plane("C")
    if own:
        fetch_codes("B", 0)
        fetch_plane("B", 0)
    fetch_c(0)

    sent, hop1 = [0], pl["hop1"]
    twin = [T.cores[r] for r in here if r != rank]
    c_to = {l: [pl["fan"][rank]] if own else hop1["%s%d" % (l, rank)] + twin for l in "Cc"}
    if own:
        early = [T.cores[r] for r in EARLY[rank]]
        g.wait_ge(S.gA, 16)
        send(g, core, T, topo, "A", rank, hop1["A%d" % rank], sent)
        g.wait_ge(S.gpA, 16)
        send(g, core, T, topo, "a", rank, hop1["a%d" % rank] + early, sent)
        send(g, core, T, topo, "A", rank, early, sent)
        g.wait_ge(S.gB, 16)
        send(g, core, T, topo, "B", rank, hop1["B%d" % rank] + twin, sent)
        g.wait_ge(S.gpB, 16)
        send(g, core, T, topo, "b", rank, hop1["b%d" % rank] + twin, sent)
    g.wait_ge(S.gC, 16)
    send(g, core, T, topo, "C", rank, c_to["C"], sent, wide=False)
    g.wait_ge(S.gpC, 16)
    send(g, core, T, topo, "c", rank, c_to["c"], sent, wide=False)
    g.wait_ge(S.sent, sent[0])

    for l in "AB":
        for k in range(1 if own else 0, G):
            fetch_codes(l, k)
            fetch_plane(l, k)
    fetch_c(1)

    ve.wait_ge(S.lx, 16)
    ve.quantize_mx(q_codes("x"), q_scales("x"), T.xt[:]).then_inc(S.xq, 1)
    for l, z, a, q, src, dst in (("A", "z", "ga", "gq", "x", "g"), ("B", "yy", "ha", "hq", "g", "h")):
        te.wait_ge(S["xq" if l == "A" else "gq"], 1)
        tile = T[dst + "t"]
        for k in range(G):
            bank = T["ps" + l][:, 512 * (k % 2):512 * (k % 2) + 128]
            if k >= 2:
                te.wait_ge(S[a + str(k - 2)], 1)
            te.wait_ge(S["vf%s%d" % (l, k)], 16)
            te.wait_ge(S["f%s%d" % (l, k)], 16)
            te.matmul_mx(bank, T["w" + l][:], plane_at(l, k), q_codes(src), q_scales(src), True, True).then_inc(S[z + str(k)], 1)
            ve.wait_ge(S[z + str(k)], 1)
            ve.tensor_scalar(tile[:, order[k]:512:4], bank, 0.0, SCALE, AluOpType.max, AluOpType.mult).then_inc(S[a + str(k)], 1)
        for k in range(G):
            ve.wait_ge(S[a + str(k)], 1)
        ve.quantize_mx(q_codes(dst), q_scales(dst), tile[:]).then_inc(S[q], 1)
    te.wait_ge(S.hq, 1)

    for j in range(N):
        bank = T.psC[:, 512 * (j % 4):512 * (j % 4) + 128]
        blk = T.yb[:, 128 * (j % 2):128 * (j % 2) + 128]
        i = c_order[j]
        te.wait_ge(S["fC%d" % j], 32)
        if j >= 4:
            te.wait_ge(S["cp%d" % (j - 4)], 1)
        te.matmul_mx(bank, T.wC[:, 128 * (j % 2):128 * (j % 2) + 128], plane_at("C", j), q_codes("h"), q_scales("h"), True,
                     True).then_inc(S["mm%d" % j], 1)
        if j + 2 < N:
            fetch_c(j + 2)
        ve.wait_ge(S["mm%d" % j], 1)
        if j >= 2:
            ve.wait_ge(S["st%d" % (j - 2)], 16)
        ve.tensor_copy(blk, bank).then_inc(S["cp%d" % j], 1)
        sc.wait_ge(S["cp%d" % j], 1)
        sc.dma_start(T.y[:, 128 * i:128 * i + 128], blk).then_inc(S["st%d" % j], 16)
    sc.wait_ge(S["st%d" % (N - 2)], 16)
    sc.wait_ge(S["st%d" % (N - 1)], 16)
